import numpy as np
import ml_dtypes


def mxq(x, axis, fmt="e4m3"):
    dtype, down = {"e4m3": (ml_dtypes.float8_e4m3fn, 7), "e5m2": (ml_dtypes.float8_e5m2, 14)}[fmt]
    v = np.moveaxis(np.asarray(x, np.float32).astype(ml_dtypes.bfloat16).astype(np.float64), axis, -1)
    blocks = v.reshape(v.shape[:-1] + (-1, 32))
    amax = np.abs(blocks).max(-1, keepdims=True)
    byte = np.maximum(np.where(amax > 0, np.frexp(amax)[1] - 1 + 127, 0) - down, 1)
    scale = np.exp2(byte - 127.0)
    codes = (blocks / scale).astype(np.float32).astype(dtype).astype(np.float64)
    return np.moveaxis((codes * scale).reshape(v.shape), -1, axis)


WIDE = False


def mx_kscale(k):
    if not WIDE:
        return np.ones(k)
    levels = np.array([10, -10, 5, -5, 0])
    if k % 512:
        return np.exp2(np.random.permutation(np.resize(levels, k // 32))).repeat(32)
    a = np.empty((k // 512, 16))
    for p in range(k // 512):
        a[p, :8] = np.random.permutation(np.resize(levels, 8))
        for g in range(8):
            far = levels[np.abs(levels - a[p, g]) >= 10]
            a[p, g + 8] = far[np.random.randint(len(far))]
    return np.exp2(a.ravel()).repeat(32)


def f64(x):
    return np.asarray(x).astype(np.float64)


def striped(idx):
    return np.tile(idx.reshape(-1, 16).T, (8, 1)).astype(np.uint16)


def unstriped(offs):
    return offs[:16].T.reshape(-1).astype(np.int64)


E2M1 = np.array([0.0, 0.5, 1.0, 1.5, 2.0, 3.0, 4.0, 6.0, -0.0, -0.5, -1.0, -1.5, -2.0, -3.0, -4.0, -6.0])


def pack_weight(w, fmt):
    k, n = w.shape
    w = f64(np.asarray(w, np.float32).astype(ml_dtypes.bfloat16)).reshape(k // 32, 32, n)
    amax = np.abs(w).max(1)
    if fmt == "e4m3":
        byte = np.frexp(amax)[1] - 1 + 127 - 7
    else:
        mant, ex = np.frexp(amax / 6.0)
        byte = np.where(mant > 0.5, ex, ex - 1) + 127
    byte = np.clip(np.where(amax > 0, byte, 1), 1, 254)
    scaled = (w * np.exp2(127.0 - byte)[:, None, :]).reshape(k, n).astype(np.float32)
    by_word = np.ascontiguousarray(scaled.reshape(k // 512, 128, 4, n).transpose(0, 1, 3, 2))
    if fmt == "e4m3":
        words = by_word.astype(ml_dtypes.float8_e4m3fn).view(np.uint8)
    else:
        c = by_word.astype(ml_dtypes.float4_e2m1fn).view(np.uint8) & 0xF
        words = (c[..., 0::2] | (c[..., 1::2] << 4)).reshape(k // 512, 128, 2 * n)
    return np.ascontiguousarray(words), np.ascontiguousarray(byte.astype(np.uint8).reshape(k // 512, 16, n))


def unpack_weight(words, scales, fmt):
    g, _, n = scales.shape
    words = np.ascontiguousarray(words).reshape(g, 128, n, -1)
    if fmt == "e4m3":
        vals = words.view(ml_dtypes.float8_e4m3fn).astype(np.float64)
    else:
        nib = np.empty((g, 128, n, 4), np.uint8)
        nib[..., 0::2] = words & 0xF
        nib[..., 1::2] = words >> 4
        vals = E2M1[nib]
    vals = vals * np.repeat(np.exp2(scales.astype(np.float64) - 127.0), 8, axis=1)[..., None]
    return vals.transpose(0, 1, 3, 2).reshape(g * 512, n)


def gelu(v):
    return 0.5 * v * (1.0 + np.tanh(np.sqrt(2.0 / np.pi) * (v + 0.044715 * v**3)))


T, S, K, H, N, P = 4096, 1024, 1024, 1536, 512, 512

def setup_inputs():
    n = np.random.standard_normal
    s = mx_kscale(K)[:, None]
    u = mx_kscale(H)[:, None]
    perm = np.random.permutation(S)
    d = {}
    d["tab_words"], d["tab_scales"] = pack_weight(n((K, T)) * s, "e2m1")
    d["offs"] = striped(np.random.permutation(T)[:S])
    d["pos1"] = striped(perm[:P])
    d["pos2"] = striped(perm[P:P + P])
    d["w1"] = (n((K, H)) / K**0.5 / s * u.T).astype(np.float32)
    d["cal"] = np.exp(0.4 * n((H, S))).astype(np.float32)
    d["w4_words"], d["w4_scales"] = pack_weight(n((H, N)) / H**0.5 / u, "e2m1")
    d["floors"] = n((N, P)).astype(np.float32)
    return d

def reference(tab_words, tab_scales, offs, pos1, pos2, w1, cal, w4_words, w4_scales, floors):
    v = unpack_weight(tab_words, tab_scales, "e2m1")[:, unstriped(offs)]
    h = (mxq(f64(w1), 0, "e4m3").T @ v) * f64(cal)
    z = h[:, unstriped(pos1)] - h[:, unstriped(pos2)]
    zq = mxq(z, 0, "e4m3")
    w4 = unpack_weight(w4_words, w4_scales, "e2m1")
    y = w4.T @ zq
    return np.maximum(y, f64(floors))

@@ -1,0 +1,240 @@
+from contextlib import ExitStack
+
+import concourse.mybir as mybir
+
+T, S, K, H, N, PAIRS = 4096, 1024, 1024, 1536, 512, 512
+FLOPS = 2 * K * H * S + 2 * H * N * PAIRS
+
+F32 = mybir.dt.float32
+BF16 = mybir.dt.bfloat16
+I32 = mybir.dt.int32
+U32 = mybir.dt.uint32
+U16 = mybir.dt.uint16
+U8 = mybir.dt.uint8
+FP8X4 = mybir.dt.float8_e4m3fn_x4
+FP4X4 = mybir.dt.float4_e2m1fn_x4
+MULT = mybir.AluOpType.mult
+SUBTRACT = mybir.AluOpType.subtract
+MAX = mybir.AluOpType.max
+
+P = 128
+PACK = 4
+PASS = P * PACK
+K_PASSES = K // PASS
+R_PASSES = H // PASS
+BANK = 512
+QUADS = 4
+SLICES = R_PASSES * PACK
+QUARTER = 128
+N_TILES = N // P
+VECTOR_COLS = 1024
+
+
+def tile_list_stereo_pair_acceptance_kernel(
+    tc, tab_words, tab_scales, offs, pos1, pos2, w1, cal, w4_words, w4_scales, floors, out
+):
+    nc = tc.nc
+    with ExitStack() as ctx:
+        keep = ctx.enter_context(tc.tile_pool(name="keep", bufs=1))
+        ring = ctx.enter_context(tc.tile_pool(name="ring", bufs=2))
+        psum_h = ctx.enter_context(tc.psum_pool(name="psum_h", bufs=2))
+        psum_y = ctx.enter_context(tc.psum_pool(name="psum_y", bufs=1))
+
+        offs_sb = keep.tile([P, S // 16], U16, name="offs_sb")
+        pos1_sb = keep.tile([P, PAIRS // 16], U16, name="pos1_sb")
+        pos2_sb = keep.tile([P, PAIRS // 16], U16, name="pos2_sb")
+        tab_scale_sb = keep.tile([P, T], U8, name="tab_scale_sb", align_bytes=64)
+        tab_word_sb = [keep.tile([P, T], U16, name="tab_word_sb%d" % a, align_bytes=64) for a in range(K_PASSES)]
+        v_words = [keep.tile([P, S], U16, name="v_words%d" % a, align_bytes=64) for a in range(K_PASSES)]
+        v_scales = [keep.tile([P, S], U8, name="v_scales%d" % a, align_bytes=64) for a in range(K_PASSES)]
+        w4_word_sb = keep.tile([P, R_PASSES, 2 * N], U8, name="w4_word_sb", align_bytes=64)
+        w4_scale_sb = keep.tile([P, R_PASSES, N], U8, name="w4_scale_sb", align_bytes=64)
+        floors_sb = keep.tile([P, N_TILES, PAIRS], F32, name="floors_sb")
+        w1_raw = {}
+        w1_codes = {}
+        w1_scales = {}
+        for b in range(R_PASSES):
+            for a in range(K_PASSES):
+                w1_raw[b, a] = keep.tile([P, PACK, PASS], F32, name="w1_raw%d%d" % (b, a))
+                w1_codes[b, a] = keep.tile([P, PASS], U32, name="w1_codes%d%d" % (b, a), align_bytes=64)
+                w1_scales[b, a] = keep.tile([P, PASS], U8, name="w1_scales%d%d" % (b, a), align_bytes=64)
+        cal_sb = [keep.tile([P, S], F32, name="cal_sb%d" % i) for i in range(SLICES)]
+        y_banks = [psum_y.tile([P, N_TILES, QUARTER], F32, name="y_bank%d" % c) for c in range(PAIRS // QUARTER)]
+
+        nc.vector.memset(tab_scale_sb[:].bitcast(I32), 0)
+        nc.vector.memset(v_scales[1][:].bitcast(I32), 0)
+        nc.vector.memset(w4_scale_sb[:].rearrange("p a n -> p (a n)").bitcast(I32), 0)
+
+        def load_w1(b, a):
+            rows = w1[a * PASS : (a + 1) * PASS, b * PASS : (b + 1) * PASS]
+            nc.sync.dma_start(out=w1_raw[b, a][:], in_=rows.rearrange("(p j) c -> p j c", j=PACK))
+
+        def load_cal(i):
+            b, t = divmod(i, PACK)
+            rows = cal[b * PASS : (b + 1) * PASS, :].rearrange("(p t) m -> p t m", t=PACK)
+            nc.sync.dma_start(out=cal_sb[i][:], in_=rows[:, t, :])
+
+        nc.sync.dma_start(offs_sb[:], offs)
+        for q in range(QUADS):
+            nc.sync.dma_start(
+                out=tab_scale_sb[32 * q : 32 * q + 4 * K_PASSES, :].bitcast(I32),
+                in_=tab_scales[:, 4 * q : 4 * q + 4, :].bitcast(I32),
+            )
+        for a in range(K_PASSES):
+            nc.sync.dma_start(out=tab_word_sb[a][:].bitcast(I32), in_=tab_words[a].bitcast(I32))
+        load_w1(0, 0)
+        load_w1(0, 1)
+        load_cal(0)
+        nc.sync.dma_start(pos2_sb[:], pos2)
+        nc.sync.dma_start(pos1_sb[:], pos1)
+        load_cal(1)
+        load_w1(1, 0)
+        load_cal(2)
+        load_w1(1, 1)
+        load_cal(3)
+        load_cal(4)
+        load_cal(5)
+        load_w1(2, 0)
+        load_cal(6)
+        load_w1(2, 1)
+        load_cal(7)
+        nc.sync.dma_start(
+            out=w4_word_sb[:].bitcast(I32), in_=w4_words.rearrange("a p n -> p a n").bitcast(I32)
+        )
+        for q in range(QUADS):
+            nc.sync.dma_start(
+                out=w4_scale_sb[32 * q : 32 * q + 4, :, :].bitcast(I32),
+                in_=w4_scales[:, 4 * q : 4 * q + 4, :].rearrange("a r n -> r a n").bitcast(I32),
+            )
+        for i in range(8, SLICES):
+            load_cal(i)
+        nc.sync.dma_start(out=floors_sb[:], in_=floors.rearrange("(u p) j -> p u j", p=P))
+
+        nc.vector.tensor_copy(v_scales[0][:], tab_scale_sb[:].indirect(offs_sb[:]))
+        for q in range(QUADS):
+            nc.scalar.dma_start(
+                out=v_scales[1][32 * q : 32 * q + 4, :].bitcast(I32),
+                in_=v_scales[0][32 * q + 4 : 32 * q + 8, :].bitcast(I32),
+            )
+        for a in range(K_PASSES):
+            nc.vector.tensor_copy(v_words[a][:], tab_word_sb[a][:].indirect(offs_sb[:]))
+
+        w1_grouped = {}
+
+        def round_w1(copy, b, a, t0, t1):
+            if (b, a) not in w1_grouped:
+                w1_grouped[b, a] = ring.tile([P, PACK * PASS], BF16, name="w1_grouped", align_bytes=64)
+            dst = w1_grouped[b, a][:].rearrange("p (t m j) -> p m j t", t=PACK, j=PACK)
+            src = w1_raw[b, a][:].rearrange("p j (m t) -> p m j t", t=PACK)
+            copy(out=dst[:, :, :, t0:t1], in_=src[:, :, :, t0:t1])
+
+        def quantize_w1(b, a, t0, t1):
+            nc.vector.quantize_mx(
+                out=w1_codes[b, a][:, t0 * P : t1 * P].bitcast(FP8X4),
+                scales=w1_scales[b, a][:, t0 * P : t1 * P],
+                in_=w1_grouped[b, a][:, t0 * PASS : t1 * PASS],
+            )
+
+        h = {}
+
+        def first_product(i):
+            b, t = divmod(i, PACK)
+            h[i] = ring.tile([P, S], F32, name="h")
+            for half in range(S // BANK):
+                bank = psum_h.tile([P, BANK], F32, name="h_bank%d" % half)
+                cols = slice(half * BANK, (half + 1) * BANK)
+                for a in range(K_PASSES):
+                    nc.tensor.matmul_mx(
+                        out=bank[:],
+                        lhsT=w1_codes[b, a][:, t * P : (t + 1) * P].bitcast(FP8X4),
+                        lhsT_scale=w1_scales[b, a][:, t * P : (t + 1) * P],
+                        rhs=v_words[a][:, cols].bitcast(FP4X4),
+                        rhs_scale=v_scales[a][:, cols],
+                        start=(a == 0),
+                        stop=(a == K_PASSES - 1),
+                    )
+                nc.vector.tensor_tensor(h[i][:, cols], bank[:], cal_sb[i][:, cols], MULT)
+
+        z = {}
+
+        def pick_pairs(i, j0, j1):
+            b, t = divmod(i, PACK)
+            if b not in z:
+                z[b] = ring.tile([P, PACK, PAIRS], F32, name="z")
+            right = ring.tile([P, j1 - j0], F32, name="right")
+            entries = slice(j0 // 16, j1 // 16)
+            nc.vector.tensor_copy(right[:], h[i][:].indirect(pos2_sb[:, entries]))
+            nc.vector.tensor_tensor(z[b][:, t, j0:j1], h[i][:].indirect(pos1_sb[:, entries]), right[:], SUBTRACT)
+
+        z_grouped = {}
+        z_codes = {}
+        z_scales = {}
+
+        def round_z(b, j0, j1):
+            z_grouped[b, j0] = ring.tile([P, PACK * (j1 - j0)], BF16, name="z_grouped", align_bytes=64)
+            nc.scalar.copy(
+                out=z_grouped[b, j0][:].rearrange("p (c i t) -> p c t i", i=4, t=PACK),
+                in_=z[b][:, :, j0:j1].rearrange("p t (c i) -> p c t i", i=4),
+            )
+
+        def quantize_z(b, j0, j1):
+            z_codes[b, j0] = ring.tile([P, j1 - j0], U32, name="z_codes", align_bytes=64)
+            z_scales[b, j0] = ring.tile([P, j1 - j0], U8, name="z_scales", align_bytes=64)
+            nc.vector.quantize_mx(
+                out=z_codes[b, j0][:].bitcast(FP8X4), scales=z_scales[b, j0][:], in_=z_grouped[b, j0][:]
+            )
+
+        def second_product(b, j0, j1):
+            for c in range(j0 // QUARTER, j1 // QUARTER):
+                cols = slice(c * QUARTER - j0, (c + 1) * QUARTER - j0)
+                for u in range(N_TILES):
+                    nc.tensor.matmul_mx(
+                        out=y_banks[c][:, u, :],
+                        lhsT=w4_word_sb[:, b, 2 * u * P : 2 * (u + 1) * P].bitcast(FP4X4),
+                        lhsT_scale=w4_scale_sb[:, b, u * P : (u + 1) * P],
+                        rhs=z_codes[b, j0][:, cols].bitcast(FP8X4),
+                        rhs_scale=z_scales[b, j0][:, cols],
+                        start=(b == 0 and u == 0),
+                        stop=(b == R_PASSES - 1 and u == N_TILES - 1),
+                    )
+
+        def finish(c):
+            cols = slice(c * QUARTER, (c + 1) * QUARTER)
+            held = keep.tile([P, N_TILES, QUARTER], F32, name="held%d" % c)
+            nc.vector.tensor_tensor(held[:], y_banks[c][:], floors_sb[:, :, cols], MAX)
+            nc.sync.dma_start(out=out.rearrange("(u p) j -> p u j", p=P)[:, :, cols], in_=held[:])
+
+        round_w1(nc.scalar.copy, 0, 0, 0, 1)
+        round_w1(nc.scalar.copy, 0, 0, 1, PACK)
+        quantize_w1(0, 0, 0, 1)
+        round_w1(nc.vector.tensor_copy, 0, 1, 0, 1)
+        quantize_w1(0, 1, 0, 1)
+        round_w1(nc.vector.tensor_copy, 0, 1, 1, PACK)
+        first_product(0)
+        quantize_w1(0, 0, 1, PACK)
+        quantize_w1(0, 1, 1, PACK)
+        last = SLICES - 1
+        for i in range(last):
+            b, t = divmod(i, PACK)
+            if b + 1 < R_PASSES and t < K_PASSES:
+                round_w1(nc.scalar.copy, b + 1, t, 0, PACK)
+            if b + 1 < R_PASSES and 1 <= t <= K_PASSES:
+                quantize_w1(b + 1, t - 1, 0, PACK)
+            first_product(i + 1)
+            pick_pairs(i, 0, PAIRS)
+            if t == PACK - 1:
+                round_z(b, 0, PAIRS)
+            if b > 0 and t == 0:
+                quantize_z(b - 1, 0, PAIRS)
+                second_product(b - 1, 0, PAIRS)
+        b = R_PASSES - 1
+        quarters = PAIRS // QUARTER
+        for step in range(quarters + 2):
+            if step < quarters:
+                pick_pairs(last, step * QUARTER, (step + 1) * QUARTER)
+                round_z(b, step * QUARTER, (step + 1) * QUARTER)
+            if 1 <= step <= quarters:
+                quantize_z(b, (step - 1) * QUARTER, step * QUARTER)
+                second_product(b, (step - 1) * QUARTER, step * QUARTER)
+            if step >= 2:
+                finish(step - 2)

@@ -27,7 +27,6 @@ QUADS = 4
 SLICES = R_PASSES * PACK
 QUARTER = 128
 N_TILES = N // P
-VECTOR_COLS = 1024
 
 
 def tile_list_stereo_pair_acceptance_kernel(
@@ -43,72 +42,60 @@ def tile_list_stereo_pair_acceptance_kernel(
         offs_sb = keep.tile([P, S // 16], U16, name="offs_sb")
         pos1_sb = keep.tile([P, PAIRS // 16], U16, name="pos1_sb")
         pos2_sb = keep.tile([P, PAIRS // 16], U16, name="pos2_sb")
-        tab_scale_sb = keep.tile([P, T], U8, name="tab_scale_sb", align_bytes=64)
-        tab_word_sb = [keep.tile([P, T], U16, name="tab_word_sb%d" % a, align_bytes=64) for a in range(K_PASSES)]
         v_words = [keep.tile([P, S], U16, name="v_words%d" % a, align_bytes=64) for a in range(K_PASSES)]
         v_scales = [keep.tile([P, S], U8, name="v_scales%d" % a, align_bytes=64) for a in range(K_PASSES)]
-        w4_word_sb = keep.tile([P, R_PASSES, 2 * N], U8, name="w4_word_sb", align_bytes=64)
-        w4_scale_sb = keep.tile([P, R_PASSES, N], U8, name="w4_scale_sb", align_bytes=64)
-        floors_sb = keep.tile([P, N_TILES, PAIRS], F32, name="floors_sb")
-        w1_raw = {}
         w1_codes = {}
         w1_scales = {}
         for b in range(R_PASSES):
             for a in range(K_PASSES):
-                w1_raw[b, a] = keep.tile([P, PACK, PASS], F32, name="w1_raw%d%d" % (b, a))
                 w1_codes[b, a] = keep.tile([P, PASS], U32, name="w1_codes%d%d" % (b, a), align_bytes=64)
                 w1_scales[b, a] = keep.tile([P, PASS], U8, name="w1_scales%d%d" % (b, a), align_bytes=64)
-        cal_sb = [keep.tile([P, S], F32, name="cal_sb%d" % i) for i in range(SLICES)]
         y_banks = [psum_y.tile([P, N_TILES, QUARTER], F32, name="y_bank%d" % c) for c in range(PAIRS // QUARTER)]
 
-        nc.vector.memset(tab_scale_sb[:].bitcast(I32), 0)
-        nc.vector.memset(v_scales[1][:].bitcast(I32), 0)
-        nc.vector.memset(w4_scale_sb[:].rearrange("p a n -> p (a n)").bitcast(I32), 0)
+        w1_raw = {}
+        cal_sb = {}
 
-        def load_w1(b, a):
+        def load_w1(b, a, tag):
+            w1_raw[b, a] = keep.tile([P, PACK, PASS], F32, name="w1_raw", tag=tag, align_bytes=64)
             rows = w1[a * PASS : (a + 1) * PASS, b * PASS : (b + 1) * PASS]
             nc.sync.dma_start(out=w1_raw[b, a][:], in_=rows.rearrange("(p j) c -> p j c", j=PACK))
 
-        def load_cal(i):
+        def load_cal(i, dst):
             b, t = divmod(i, PACK)
             rows = cal[b * PASS : (b + 1) * PASS, :].rearrange("(p t) m -> p t m", t=PACK)
-            nc.sync.dma_start(out=cal_sb[i][:], in_=rows[:, t, :])
+            nc.sync.dma_start(out=dst, in_=rows[:, t, :])
+            cal_sb[i] = dst
 
+        def load_cal_alone(i, tag):
+            tile = keep.tile([P, S], F32, name="cal_alone", tag=tag, align_bytes=64)
+            load_cal(i, tile[:])
+
+        page = {}
+
+        def load_page(b, tag):
+            page[b] = keep.tile([P, PACK, S], F32, name="page", tag=tag, align_bytes=64)
+            for t in range(PACK):
+                i = PACK * b + t + 1
+                if 2 <= i < SLICES:
+                    load_cal(i, page[b][:, t, :])
+
+        tab_scale_sb = keep.tile([P, T], U8, name="tab_scale_sb", tag="first", align_bytes=64)
+        nc.vector.memset(tab_scale_sb[:].bitcast(I32), 0)
+        nc.vector.memset(v_scales[1][:].bitcast(I32), 0)
         nc.sync.dma_start(offs_sb[:], offs)
+        nc.sync.dma_start(pos2_sb[:], pos2)
+        nc.sync.dma_start(pos1_sb[:], pos1)
         for q in range(QUADS):
             nc.sync.dma_start(
                 out=tab_scale_sb[32 * q : 32 * q + 4 * K_PASSES, :].bitcast(I32),
                 in_=tab_scales[:, 4 * q : 4 * q + 4, :].bitcast(I32),
             )
+        tab_word_sb = []
         for a in range(K_PASSES):
+            tab_word_sb.append(keep.tile([P, T], U16, name="tab_word_sb", tag="AB"[a], align_bytes=64))
             nc.sync.dma_start(out=tab_word_sb[a][:].bitcast(I32), in_=tab_words[a].bitcast(I32))
-        load_w1(0, 0)
-        load_w1(0, 1)
-        load_cal(0)
-        nc.sync.dma_start(pos2_sb[:], pos2)
-        nc.sync.dma_start(pos1_sb[:], pos1)
-        load_cal(1)
-        load_w1(1, 0)
-        load_cal(2)
-        load_w1(1, 1)
-        load_cal(3)
-        load_cal(4)
-        load_cal(5)
-        load_w1(2, 0)
-        load_cal(6)
-        load_w1(2, 1)
-        load_cal(7)
-        nc.sync.dma_start(
-            out=w4_word_sb[:].bitcast(I32), in_=w4_words.rearrange("a p n -> p a n").bitcast(I32)
-        )
-        for q in range(QUADS):
-            nc.sync.dma_start(
-                out=w4_scale_sb[32 * q : 32 * q + 4, :, :].bitcast(I32),
-                in_=w4_scales[:, 4 * q : 4 * q + 4, :].rearrange("a r n -> r a n").bitcast(I32),
-            )
-        for i in range(8, SLICES):
-            load_cal(i)
-        nc.sync.dma_start(out=floors_sb[:], in_=floors.rearrange("(u p) j -> p u j", p=P))
+        load_w1(0, 0, "C")
+        load_w1(0, 1, "D")
 
         nc.vector.tensor_copy(v_scales[0][:], tab_scale_sb[:].indirect(offs_sb[:]))
         for q in range(QUADS):
@@ -122,7 +109,9 @@ def tile_list_stereo_pair_acceptance_kernel(
         w1_grouped = {}
 
         def round_w1(copy, b, a, t0, t1):
-            if (b, a) not in w1_grouped:
+            if (b, a) == (0, 1) and t0 == 0:
+                w1_grouped[b, a] = keep.tile([P, PACK * PASS], BF16, name="w1_grouped01", tag="second", align_bytes=64)
+            elif t0 == 0:
                 w1_grouped[b, a] = ring.tile([P, PACK * PASS], BF16, name="w1_grouped", align_bytes=64)
             dst = w1_grouped[b, a][:].rearrange("p (t m j) -> p m j t", t=PACK, j=PACK)
             src = w1_raw[b, a][:].rearrange("p j (m t) -> p m j t", t=PACK)
@@ -155,36 +144,43 @@ def tile_list_stereo_pair_acceptance_kernel(
                     )
                 nc.vector.tensor_tensor(h[i][:, cols], bank[:], cal_sb[i][:, cols], MULT)
 
-        z = {}
+        right = {}
 
-        def pick_pairs(i, j0, j1):
+        def pick_right(i, j0, j1):
+            if j0 == PAIRS - QUARTER:
+                right[i, j0] = keep.tile([P, j1 - j0], F32, name="right_last", tag="tail", align_bytes=64)
+            else:
+                right[i, j0] = ring.tile([P, j1 - j0], F32, name="right", bufs=3)
+            nc.vector.tensor_copy(right[i, j0][:], h[i][:].indirect(pos2_sb[:, j0 // 16 : j1 // 16]))
+
+        def pick_left(i, j0, j1):
             b, t = divmod(i, PACK)
-            if b not in z:
-                z[b] = ring.tile([P, PACK, PAIRS], F32, name="z")
-            right = ring.tile([P, j1 - j0], F32, name="right")
-            entries = slice(j0 // 16, j1 // 16)
-            nc.vector.tensor_copy(right[:], h[i][:].indirect(pos2_sb[:, entries]))
-            nc.vector.tensor_tensor(z[b][:, t, j0:j1], h[i][:].indirect(pos1_sb[:, entries]), right[:], SUBTRACT)
+            nc.vector.tensor_tensor(
+                page[b][:, t, j0:j1], h[i][:].indirect(pos1_sb[:, j0 // 16 : j1 // 16]), right[i, j0][:], SUBTRACT
+            )
 
         z_grouped = {}
         z_codes = {}
         z_scales = {}
 
         def round_z(b, j0, j1):
-            z_grouped[b, j0] = ring.tile([P, PACK * (j1 - j0)], BF16, name="z_grouped", align_bytes=64)
+            if (b, j0) == (R_PASSES - 1, 0):
+                z_grouped[b, j0] = keep.tile([P, PACK * (j1 - j0)], BF16, name="z_first", tag="tail", align_bytes=64)
+            else:
+                z_grouped[b, j0] = ring.tile([P, PACK * (j1 - j0)], BF16, name="z_grouped", bufs=3, align_bytes=64)
             nc.scalar.copy(
                 out=z_grouped[b, j0][:].rearrange("p (c i t) -> p c t i", i=4, t=PACK),
-                in_=z[b][:, :, j0:j1].rearrange("p t (c i) -> p c t i", i=4),
+                in_=page[b][:, :, j0:j1].rearrange("p t (c i) -> p c t i", i=4),
             )
 
         def quantize_z(b, j0, j1):
-            z_codes[b, j0] = ring.tile([P, j1 - j0], U32, name="z_codes", align_bytes=64)
-            z_scales[b, j0] = ring.tile([P, j1 - j0], U8, name="z_scales", align_bytes=64)
+            z_codes[b, j0] = ring.tile([P, j1 - j0], U32, name="z_codes", bufs=4, align_bytes=64)
+            z_scales[b, j0] = ring.tile([P, j1 - j0], U8, name="z_scales", bufs=4, align_bytes=64)
             nc.vector.quantize_mx(
                 out=z_codes[b, j0][:].bitcast(FP8X4), scales=z_scales[b, j0][:], in_=z_grouped[b, j0][:]
             )
 
-        def second_product(b, j0, j1):
+        def second_product(b, j0, j1, w4_word_sb, w4_scale_sb):
             for c in range(j0 // QUARTER, j1 // QUARTER):
                 cols = slice(c * QUARTER - j0, (c + 1) * QUARTER - j0)
                 for u in range(N_TILES):
@@ -198,43 +194,74 @@ def tile_list_stereo_pair_acceptance_kernel(
                         stop=(b == R_PASSES - 1 and u == N_TILES - 1),
                     )
 
-        def finish(c):
+        def finish(c, floors_sb):
             cols = slice(c * QUARTER, (c + 1) * QUARTER)
             held = keep.tile([P, N_TILES, QUARTER], F32, name="held%d" % c)
             nc.vector.tensor_tensor(held[:], y_banks[c][:], floors_sb[:, :, cols], MAX)
             nc.sync.dma_start(out=out.rearrange("(u p) j -> p u j", p=P)[:, :, cols], in_=held[:])
 
+        load_cal_alone(0, "first")
+        load_cal_alone(1, "A")
+        load_w1(1, 0, "B")
         round_w1(nc.scalar.copy, 0, 0, 0, 1)
         round_w1(nc.scalar.copy, 0, 0, 1, PACK)
         quantize_w1(0, 0, 0, 1)
         round_w1(nc.vector.tensor_copy, 0, 1, 0, 1)
         quantize_w1(0, 1, 0, 1)
-        round_w1(nc.vector.tensor_copy, 0, 1, 1, PACK)
-        first_product(0)
+        round_w1(nc.vector.tensor_copy, 0, 1, 1, 2)
+        round_w1(nc.scalar.copy, 0, 1, 2, PACK)
         quantize_w1(0, 0, 1, PACK)
-        quantize_w1(0, 1, 1, PACK)
+        quantize_w1(0, 1, 1, 2)
+        first_product(0)
+        quantize_w1(0, 1, 2, PACK)
+        load_w1(1, 1, "C")
+        load_page(0, "D")
+        pick_right(0, 0, PAIRS)
+
+        w4_word_sb = keep.tile([P, R_PASSES, 2 * N], U8, name="w4_word_sb", tag="first", align_bytes=64)
+        nc.sync.dma_start(out=w4_word_sb[:].bitcast(I32), in_=w4_words.rearrange("a p n -> p a n").bitcast(I32))
+        w4_scale_sb = keep.tile([P, R_PASSES, N], U8, name="w4_scale_sb", tag="second", align_bytes=64)
+        nc.gpsimd.memset(w4_scale_sb[:].rearrange("p a n -> p (a n)").bitcast(I32), 0)
+        for q in range(QUADS):
+            nc.sync.dma_start(
+                out=w4_scale_sb[32 * q : 32 * q + 4, :, :].bitcast(I32),
+                in_=w4_scales[:, 4 * q : 4 * q + 4, :].rearrange("a r n -> r a n").bitcast(I32),
+            )
+
         last = SLICES - 1
         for i in range(last):
             b, t = divmod(i, PACK)
+            if i == 1:
+                load_w1(2, 1, "A")
+                load_w1(2, 0, "B")
+            if i == 2:
+                load_page(1, "C")
+            if i == 4:
+                load_page(2, "D")
             if b + 1 < R_PASSES and t < K_PASSES:
                 round_w1(nc.scalar.copy, b + 1, t, 0, PACK)
             if b + 1 < R_PASSES and 1 <= t <= K_PASSES:
                 quantize_w1(b + 1, t - 1, 0, PACK)
             first_product(i + 1)
-            pick_pairs(i, 0, PAIRS)
+            pick_left(i, 0, PAIRS)
+            pick_right(i + 1, 0, PAIRS if i + 1 < last else QUARTER)
             if t == PACK - 1:
                 round_z(b, 0, PAIRS)
             if b > 0 and t == 0:
                 quantize_z(b - 1, 0, PAIRS)
-                second_product(b - 1, 0, PAIRS)
+                second_product(b - 1, 0, PAIRS, w4_word_sb, w4_scale_sb)
+        floors_sb = keep.tile([P, N_TILES, PAIRS], F32, name="floors_sb", tag="B", align_bytes=64)
+        nc.sync.dma_start(out=floors_sb[:], in_=floors.rearrange("(u p) j -> p u j", p=P))
         b = R_PASSES - 1
         quarters = PAIRS // QUARTER
         for step in range(quarters + 2):
+            if step + 1 < quarters:
+                pick_right(last, (step + 1) * QUARTER, (step + 2) * QUARTER)
             if step < quarters:
-                pick_pairs(last, step * QUARTER, (step + 1) * QUARTER)
+                pick_left(last, step * QUARTER, (step + 1) * QUARTER)
                 round_z(b, step * QUARTER, (step + 1) * QUARTER)
             if 1 <= step <= quarters:
                 quantize_z(b, (step - 1) * QUARTER, step * QUARTER)
-                second_product(b, (step - 1) * QUARTER, step * QUARTER)
+                second_product(b, (step - 1) * QUARTER, step * QUARTER, w4_word_sb, w4_scale_sb)
             if step >= 2:
-                finish(step - 2)
+                finish(step - 2, floors_sb)

@@ -55,29 +55,16 @@ def tile_list_stereo_pair_acceptance_kernel(
         w1_raw = {}
         cal_sb = {}
 
-        def load_w1(b, a, tag):
-            w1_raw[b, a] = keep.tile([P, PACK, PASS], F32, name="w1_raw", tag=tag, align_bytes=64)
+        def load_w1(b, a, dst):
+            w1_raw[b, a] = dst.rearrange("p (j c) -> p j c", j=PACK)
             rows = w1[a * PASS : (a + 1) * PASS, b * PASS : (b + 1) * PASS]
-            nc.sync.dma_start(out=w1_raw[b, a][:], in_=rows.rearrange("(p j) c -> p j c", j=PACK))
+            nc.sync.dma_start(out=w1_raw[b, a], in_=rows.rearrange("(p j) c -> p j c", j=PACK))
 
         def load_cal(i, dst):
             b, t = divmod(i, PACK)
+            cal_sb[i] = dst
             rows = cal[b * PASS : (b + 1) * PASS, :].rearrange("(p t) m -> p t m", t=PACK)
             nc.sync.dma_start(out=dst, in_=rows[:, t, :])
-            cal_sb[i] = dst
-
-        def load_cal_alone(i, tag):
-            tile = keep.tile([P, S], F32, name="cal_alone", tag=tag, align_bytes=64)
-            load_cal(i, tile[:])
-
-        page = {}
-
-        def load_page(b, tag):
-            page[b] = keep.tile([P, PACK, S], F32, name="page", tag=tag, align_bytes=64)
-            for t in range(PACK):
-                i = PACK * b + t + 1
-                if 2 <= i < SLICES:
-                    load_cal(i, page[b][:, t, :])
 
         tab_scale_sb = keep.tile([P, T], U8, name="tab_scale_sb", tag="first", align_bytes=64)
         nc.vector.memset(tab_scale_sb[:].bitcast(I32), 0)
@@ -92,10 +79,10 @@ def tile_list_stereo_pair_acceptance_kernel(
             )
         tab_word_sb = []
         for a in range(K_PASSES):
-            tab_word_sb.append(keep.tile([P, T], U16, name="tab_word_sb", tag="AB"[a], align_bytes=64))
+            tab_word_sb.append(keep.tile([P, T], U16, name="tab_word_sb", tag="words%d" % a, align_bytes=64))
             nc.sync.dma_start(out=tab_word_sb[a][:].bitcast(I32), in_=tab_words[a].bitcast(I32))
-        load_w1(0, 0, "C")
-        load_w1(0, 1, "D")
+        for a in range(K_PASSES):
+            load_w1(0, a, keep.tile([P, PACK * PASS], F32, name="w1_first%d" % a)[:])
 
         nc.vector.tensor_copy(v_scales[0][:], tab_scale_sb[:].indirect(offs_sb[:]))
         for q in range(QUADS):
@@ -109,12 +96,12 @@ def tile_list_stereo_pair_acceptance_kernel(
         w1_grouped = {}
 
         def round_w1(copy, b, a, t0, t1):
-            if (b, a) == (0, 1) and t0 == 0:
-                w1_grouped[b, a] = keep.tile([P, PACK * PASS], BF16, name="w1_grouped01", tag="second", align_bytes=64)
+            if b == 1 and t0 == 0:
+                w1_grouped[b, a] = keep.tile([P, PACK * PASS], BF16, name="w1_mid", tag="mid%d" % a, align_bytes=64)
             elif t0 == 0:
                 w1_grouped[b, a] = ring.tile([P, PACK * PASS], BF16, name="w1_grouped", align_bytes=64)
             dst = w1_grouped[b, a][:].rearrange("p (t m j) -> p m j t", t=PACK, j=PACK)
-            src = w1_raw[b, a][:].rearrange("p j (m t) -> p m j t", t=PACK)
+            src = w1_raw[b, a].rearrange("p j (m t) -> p m j t", t=PACK)
             copy(out=dst[:, :, :, t0:t1], in_=src[:, :, :, t0:t1])
 
         def quantize_w1(b, a, t0, t1):
@@ -124,12 +111,12 @@ def tile_list_stereo_pair_acceptance_kernel(
                 in_=w1_grouped[b, a][:, t0 * PASS : t1 * PASS],
             )
 
-        h = {}
+        h_tiles = [keep.tile([P, S], F32, name="h%d" % n) for n in range(2)]
+        h = [h_tiles[i % 2] for i in range(SLICES)]
 
         def first_product(i):
             b, t = divmod(i, PACK)
-            h[i] = ring.tile([P, S], F32, name="h")
-            for half in range(S // BANK):
+            for half in reversed(range(S // BANK)):
                 bank = psum_h.tile([P, BANK], F32, name="h_bank%d" % half)
                 cols = slice(half * BANK, (half + 1) * BANK)
                 for a in range(K_PASSES):
@@ -142,21 +129,25 @@ def tile_list_stereo_pair_acceptance_kernel(
                         start=(a == 0),
                         stop=(a == K_PASSES - 1),
                     )
-                nc.vector.tensor_tensor(h[i][:, cols], bank[:], cal_sb[i][:, cols], MULT)
+                if half == 0 or i == 0:
+                    nc.vector.tensor_tensor(h[i][:, cols], bank[:], cal_sb[i][:, cols], MULT)
+                else:
+                    sums = ring.tile([P, BANK], F32, name="sums")
+                    nc.scalar.copy(out=sums[:], in_=bank[:])
+                    nc.gpsimd.tensor_tensor(h[i][:, cols], sums[:], cal_sb[i][:, cols], MULT)
 
         right = {}
 
         def pick_right(i, j0, j1):
             if j0 == PAIRS - QUARTER:
-                right[i, j0] = keep.tile([P, j1 - j0], F32, name="right_last", tag="tail", align_bytes=64)
+                right[i, j0] = keep.tile([P, j1 - j0], F32, name="right_last", tag="tail", align_bytes=64)[:]
             else:
-                right[i, j0] = ring.tile([P, j1 - j0], F32, name="right", bufs=3)
-            nc.vector.tensor_copy(right[i, j0][:], h[i][:].indirect(pos2_sb[:, j0 // 16 : j1 // 16]))
+                right[i, j0] = ring.tile([P, j1 - j0], F32, name="right", bufs=3)[:]
+            nc.vector.tensor_copy(right[i, j0], h[i][:].indirect(pos2_sb[:, j0 // 16 : j1 // 16]))
 
         def pick_left(i, j0, j1):
-            b, t = divmod(i, PACK)
             nc.vector.tensor_tensor(
-                page[b][:, t, j0:j1], h[i][:].indirect(pos1_sb[:, j0 // 16 : j1 // 16]), right[i, j0][:], SUBTRACT
+                pages[:, i * S + j0 : i * S + j1], h[i][:].indirect(pos1_sb[:, j0 // 16 : j1 // 16]), right[i, j0], SUBTRACT
             )
 
         z_grouped = {}
@@ -170,7 +161,9 @@ def tile_list_stereo_pair_acceptance_kernel(
                 z_grouped[b, j0] = ring.tile([P, PACK * (j1 - j0)], BF16, name="z_grouped", bufs=3, align_bytes=64)
             nc.scalar.copy(
                 out=z_grouped[b, j0][:].rearrange("p (c i t) -> p c t i", i=4, t=PACK),
-                in_=page[b][:, :, j0:j1].rearrange("p t (c i) -> p c t i", i=4),
+                in_=pages[:, PACK * b * S : PACK * (b + 1) * S]
+                .rearrange("p (t m) -> p t m", t=PACK)[:, :, j0:j1]
+                .rearrange("p t (c i) -> p c t i", i=4),
             )
 
         def quantize_z(b, j0, j1):
@@ -200,9 +193,20 @@ def tile_list_stereo_pair_acceptance_kernel(
             nc.vector.tensor_tensor(held[:], y_banks[c][:], floors_sb[:, :, cols], MAX)
             nc.sync.dma_start(out=out.rearrange("(u p) j -> p u j", p=P)[:, :, cols], in_=held[:])
 
-        load_cal_alone(0, "first")
-        load_cal_alone(1, "A")
-        load_w1(1, 0, "B")
+        load_cal(0, keep.tile([P, S], F32, name="cal_first", tag="first", align_bytes=64)[:])
+        pages = keep.tile([P, SLICES * S], F32, name="pages", tag="words0", align_bytes=64)
+        w1_rest = keep.tile(
+            [P, (R_PASSES - 1) * K_PASSES * PACK * PASS + N_TILES * PAIRS], F32, name="w1_rest", tag="words1", align_bytes=64
+        )
+        for i in range(1, SLICES):
+            b, t = divmod(i, PACK)
+            if b + 1 < R_PASSES and t == PACK - 1:
+                for a in range(K_PASSES):
+                    n = b * K_PASSES + a
+                    load_w1(b + 1, a, w1_rest[:, n * PACK * PASS : (n + 1) * PACK * PASS])
+            load_cal(i, pages[:, (i - 1) * S : i * S])
+        floors_sb = w1_rest[:, (R_PASSES - 1) * K_PASSES * PACK * PASS :].rearrange("p (u j) -> p u j", u=N_TILES)
+        nc.sync.dma_start(out=floors_sb, in_=floors.rearrange("(u p) j -> p u j", p=P))
         round_w1(nc.scalar.copy, 0, 0, 0, 1)
         round_w1(nc.scalar.copy, 0, 0, 1, PACK)
         quantize_w1(0, 0, 0, 1)
@@ -213,45 +217,42 @@ def tile_list_stereo_pair_acceptance_kernel(
         quantize_w1(0, 0, 1, PACK)
         quantize_w1(0, 1, 1, 2)
         first_product(0)
-        quantize_w1(0, 1, 2, PACK)
-        load_w1(1, 1, "C")
-        load_page(0, "D")
         pick_right(0, 0, PAIRS)
-
-        w4_word_sb = keep.tile([P, R_PASSES, 2 * N], U8, name="w4_word_sb", tag="first", align_bytes=64)
-        nc.sync.dma_start(out=w4_word_sb[:].bitcast(I32), in_=w4_words.rearrange("a p n -> p a n").bitcast(I32))
-        w4_scale_sb = keep.tile([P, R_PASSES, N], U8, name="w4_scale_sb", tag="second", align_bytes=64)
-        nc.gpsimd.memset(w4_scale_sb[:].rearrange("p a n -> p (a n)").bitcast(I32), 0)
-        for q in range(QUADS):
-            nc.sync.dma_start(
-                out=w4_scale_sb[32 * q : 32 * q + 4, :, :].bitcast(I32),
-                in_=w4_scales[:, 4 * q : 4 * q + 4, :].rearrange("a r n -> r a n").bitcast(I32),
-            )
+        quantize_w1(0, 1, 2, PACK)
 
         last = SLICES - 1
         for i in range(last):
             b, t = divmod(i, PACK)
-            if i == 1:
-                load_w1(2, 1, "A")
-                load_w1(2, 0, "B")
-            if i == 2:
-                load_page(1, "C")
-            if i == 4:
-                load_page(2, "D")
-            if b + 1 < R_PASSES and t < K_PASSES:
-                round_w1(nc.scalar.copy, b + 1, t, 0, PACK)
-            if b + 1 < R_PASSES and 1 <= t <= K_PASSES:
-                quantize_w1(b + 1, t - 1, 0, PACK)
+            if b + 1 < R_PASSES and t == 0:
+                round_w1(nc.scalar.copy, b + 1, 0, 0, PACK)
+            if b + 1 < R_PASSES and t == 1:
+                quantize_w1(b + 1, 0, 0, PACK)
+                round_w1(nc.scalar.copy, b + 1, 1, 0, 1)
+                round_w1(nc.scalar.copy, b + 1, 1, 1, PACK)
+            if b + 1 < R_PASSES and t == 2:
+                quantize_w1(b + 1, 1, 0, 1)
+            if b + 1 < R_PASSES and t == 3:
+                quantize_w1(b + 1, 1, 1, PACK)
+            if b > 0 and t == 1:
+                quantize_z(b - 1, 0, PAIRS)
+                second_product(b - 1, 0, PAIRS, w4_word_sb, w4_scale_sb)
             first_product(i + 1)
             pick_left(i, 0, PAIRS)
             pick_right(i + 1, 0, PAIRS if i + 1 < last else QUARTER)
             if t == PACK - 1:
                 round_z(b, 0, PAIRS)
-            if b > 0 and t == 0:
-                quantize_z(b - 1, 0, PAIRS)
-                second_product(b - 1, 0, PAIRS, w4_word_sb, w4_scale_sb)
-        floors_sb = keep.tile([P, N_TILES, PAIRS], F32, name="floors_sb", tag="B", align_bytes=64)
-        nc.sync.dma_start(out=floors_sb[:], in_=floors.rearrange("(u p) j -> p u j", p=P))
+            if i == PACK - 1:
+                w4_word_sb = keep.tile([P, R_PASSES, 2 * N], U8, name="w4_word_sb", tag="mid0", align_bytes=64)
+                nc.sync.dma_start(
+                    out=w4_word_sb[:].bitcast(I32), in_=w4_words.rearrange("a p n -> p a n").bitcast(I32)
+                )
+                w4_scale_sb = keep.tile([P, R_PASSES, N], U8, name="w4_scale_sb", tag="mid1", align_bytes=64)
+                nc.gpsimd.memset(w4_scale_sb[:].rearrange("p a n -> p (a n)").bitcast(I32), 0)
+                for q in range(QUADS):
+                    nc.sync.dma_start(
+                        out=w4_scale_sb[32 * q : 32 * q + 4, :, :].bitcast(I32),
+                        in_=w4_scales[:, 4 * q : 4 * q + 4, :].rearrange("a r n -> r a n").bitcast(I32),
+                    )
         b = R_PASSES - 1
         quarters = PAIRS // QUARTER
         for step in range(quarters + 2):

@@ -27,6 +27,7 @@ QUADS = 4
 SLICES = R_PASSES * PACK
 QUARTER = 128
 N_TILES = N // P
+LEAD = 256
 
 
 def tile_list_stereo_pair_acceptance_kernel(
@@ -129,8 +130,11 @@ def tile_list_stereo_pair_acceptance_kernel(
                         start=(a == 0),
                         stop=(a == K_PASSES - 1),
                     )
-                if half == 0 or i == 0:
+                if i == 0:
                     nc.vector.tensor_tensor(h[i][:, cols], bank[:], cal_sb[i][:, cols], MULT)
+                elif half == 0:
+                    for part in (slice(0, LEAD), slice(LEAD, BANK)):
+                        nc.vector.tensor_tensor(h[i][:, part], bank[:, part], cal_sb[i][:, part], MULT)
                 else:
                     sums = ring.tile([P, BANK], F32, name="sums")
                     nc.scalar.copy(out=sums[:], in_=bank[:])
@@ -204,7 +208,7 @@ def tile_list_stereo_pair_acceptance_kernel(
                 for a in range(K_PASSES):
                     n = b * K_PASSES + a
                     load_w1(b + 1, a, w1_rest[:, n * PACK * PASS : (n + 1) * PACK * PASS])
-            load_cal(i, pages[:, (i - 1) * S : i * S])
+            load_cal(i, pages[:, LEAD + (i - 1) * S : LEAD + i * S])
         floors_sb = w1_rest[:, (R_PASSES - 1) * K_PASSES * PACK * PASS :].rearrange("p (u j) -> p u j", u=N_TILES)
         nc.sync.dma_start(out=floors_sb, in_=floors.rearrange("(u p) j -> p u j", p=P))
         round_w1(nc.scalar.copy, 0, 0, 0, 1)

from contextlib import ExitStack

import concourse.mybir as mybir

T, S, K, H, N, PAIRS = 4096, 1024, 1024, 1536, 512, 512
FLOPS = 2 * K * H * S + 2 * H * N * PAIRS

F32 = mybir.dt.float32
BF16 = mybir.dt.bfloat16
I32 = mybir.dt.int32
U32 = mybir.dt.uint32
U16 = mybir.dt.uint16
U8 = mybir.dt.uint8
FP8X4 = mybir.dt.float8_e4m3fn_x4
FP4X4 = mybir.dt.float4_e2m1fn_x4
MULT = mybir.AluOpType.mult
SUBTRACT = mybir.AluOpType.subtract
MAX = mybir.AluOpType.max

P = 128
PACK = 4
PASS = P * PACK
K_PASSES = K // PASS
R_PASSES = H // PASS
BANK = 512
QUADS = 4
SLICES = R_PASSES * PACK
QUARTER = 128
N_TILES = N // P
LEAD = 256


def tile_list_stereo_pair_acceptance_kernel(
    tc, tab_words, tab_scales, offs, pos1, pos2, w1, cal, w4_words, w4_scales, floors, out
):
    nc = tc.nc
    with ExitStack() as ctx:
        keep = ctx.enter_context(tc.tile_pool(name="keep", bufs=1))
        ring = ctx.enter_context(tc.tile_pool(name="ring", bufs=2))
        psum_h = ctx.enter_context(tc.psum_pool(name="psum_h", bufs=2))
        psum_y = ctx.enter_context(tc.psum_pool(name="psum_y", bufs=1))

        offs_sb = keep.tile([P, S // 16], U16, name="offs_sb")
        pos1_sb = keep.tile([P, PAIRS // 16], U16, name="pos1_sb")
        pos2_sb = keep.tile([P, PAIRS // 16], U16, name="pos2_sb")
        v_words = [keep.tile([P, S], U16, name="v_words%d" % a, align_bytes=64) for a in range(K_PASSES)]
        v_scales = [keep.tile([P, S], U8, name="v_scales%d" % a, align_bytes=64) for a in range(K_PASSES)]
        w1_codes = {}
        w1_scales = {}
        for b in range(R_PASSES):
            for a in range(K_PASSES):
                w1_codes[b, a] = keep.tile([P, PASS], U32, name="w1_codes%d%d" % (b, a), align_bytes=64)
                w1_scales[b, a] = keep.tile([P, PASS], U8, name="w1_scales%d%d" % (b, a), align_bytes=64)
        y_banks = [psum_y.tile([P, N_TILES, QUARTER], F32, name="y_bank%d" % c) for c in range(PAIRS // QUARTER)]

        w1_raw = {}
        cal_sb = {}

        def load_w1(b, a, dst):
            w1_raw[b, a] = dst.rearrange("p (j c) -> p j c", j=PACK)
            rows = w1[a * PASS : (a + 1) * PASS, b * PASS : (b + 1) * PASS]
            nc.sync.dma_start(out=w1_raw[b, a], in_=rows.rearrange("(p j) c -> p j c", j=PACK))

        def load_cal(i, dst):
            b, t = divmod(i, PACK)
            cal_sb[i] = dst
            rows = cal[b * PASS : (b + 1) * PASS, :].rearrange("(p t) m -> p t m", t=PACK)
            nc.sync.dma_start(out=dst, in_=rows[:, t, :])

        tab_scale_sb = keep.tile([P, T], U8, name="tab_scale_sb", tag="first", align_bytes=64)
        nc.vector.memset(tab_scale_sb[:].bitcast(I32), 0)
        nc.vector.memset(v_scales[1][:].bitcast(I32), 0)
        nc.sync.dma_start(offs_sb[:], offs)
        nc.sync.dma_start(pos2_sb[:], pos2)
        nc.sync.dma_start(pos1_sb[:], pos1)
        for q in range(QUADS):
            nc.sync.dma_start(
                out=tab_scale_sb[32 * q : 32 * q + 4 * K_PASSES, :].bitcast(I32),
                in_=tab_scales[:, 4 * q : 4 * q + 4, :].bitcast(I32),
            )
        tab_word_sb = []
        for a in range(K_PASSES):
            tab_word_sb.append(keep.tile([P, T], U16, name="tab_word_sb", tag="words%d" % a, align_bytes=64))
            nc.sync.dma_start(out=tab_word_sb[a][:].bitcast(I32), in_=tab_words[a].bitcast(I32))
        for a in range(K_PASSES):
            load_w1(0, a, keep.tile([P, PACK * PASS], F32, name="w1_first%d" % a)[:])

        nc.vector.tensor_copy(v_scales[0][:], tab_scale_sb[:].indirect(offs_sb[:]))
        for q in range(QUADS):
            nc.scalar.dma_start(
                out=v_scales[1][32 * q : 32 * q + 4, :].bitcast(I32),
                in_=v_scales[0][32 * q + 4 : 32 * q + 8, :].bitcast(I32),
            )
        for a in range(K_PASSES):
            nc.vector.tensor_copy(v_words[a][:], tab_word_sb[a][:].indirect(offs_sb[:]))

        w1_grouped = {}

        def round_w1(copy, b, a, t0, t1):
            if b == 1 and t0 == 0:
                w1_grouped[b, a] = keep.tile([P, PACK * PASS], BF16, name="w1_mid", tag="mid%d" % a, align_bytes=64)
            elif t0 == 0:
                w1_grouped[b, a] = ring.tile([P, PACK * PASS], BF16, name="w1_grouped", align_bytes=64)
            dst = w1_grouped[b, a][:].rearrange("p (t m j) -> p m j t", t=PACK, j=PACK)
            src = w1_raw[b, a].rearrange("p j (m t) -> p m j t", t=PACK)
            copy(out=dst[:, :, :, t0:t1], in_=src[:, :, :, t0:t1])

        def quantize_w1(b, a, t0, t1):
            nc.vector.quantize_mx(
                out=w1_codes[b, a][:, t0 * P : t1 * P].bitcast(FP8X4),
                scales=w1_scales[b, a][:, t0 * P : t1 * P],
                in_=w1_grouped[b, a][:, t0 * PASS : t1 * PASS],
            )

        h_tiles = [keep.tile([P, S], F32, name="h%d" % n) for n in range(2)]
        h = [h_tiles[i % 2] for i in range(SLICES)]

        def first_product(i):
            b, t = divmod(i, PACK)
            for half in reversed(range(S // BANK)):
                bank = psum_h.tile([P, BANK], F32, name="h_bank%d" % half)
                cols = slice(half * BANK, (half + 1) * BANK)
                for a in range(K_PASSES):
                    nc.tensor.matmul_mx(
                        out=bank[:],
                        lhsT=w1_codes[b, a][:, t * P : (t + 1) * P].bitcast(FP8X4),
                        lhsT_scale=w1_scales[b, a][:, t * P : (t + 1) * P],
                        rhs=v_words[a][:, cols].bitcast(FP4X4),
                        rhs_scale=v_scales[a][:, cols],
                        start=(a == 0),
                        stop=(a == K_PASSES - 1),
                    )
                if i == 0:
                    nc.vector.tensor_tensor(h[i][:, cols], bank[:], cal_sb[i][:, cols], MULT)
                elif half == 0:
                    for part in (slice(0, LEAD), slice(LEAD, BANK)):
                        nc.vector.tensor_tensor(h[i][:, part], bank[:, part], cal_sb[i][:, part], MULT)
                else:
                    sums = ring.tile([P, BANK], F32, name="sums")
                    nc.scalar.copy(out=sums[:], in_=bank[:])
                    nc.gpsimd.tensor_tensor(h[i][:, cols], sums[:], cal_sb[i][:, cols], MULT)

        right = {}

        def pick_right(i, j0, j1):
            if j0 == PAIRS - QUARTER:
                right[i, j0] = keep.tile([P, j1 - j0], F32, name="right_last", tag="tail", align_bytes=64)[:]
            else:
                right[i, j0] = ring.tile([P, j1 - j0], F32, name="right", bufs=3)[:]
            nc.vector.tensor_copy(right[i, j0], h[i][:].indirect(pos2_sb[:, j0 // 16 : j1 // 16]))

        def pick_left(i, j0, j1):
            nc.vector.tensor_tensor(
                pages[:, i * S + j0 : i * S + j1], h[i][:].indirect(pos1_sb[:, j0 // 16 : j1 // 16]), right[i, j0], SUBTRACT
            )

        z_grouped = {}
        z_codes = {}
        z_scales = {}

        def round_z(b, j0, j1):
            if (b, j0) == (R_PASSES - 1, 0):
                z_grouped[b, j0] = keep.tile([P, PACK * (j1 - j0)], BF16, name="z_first", tag="tail", align_bytes=64)
            else:
                z_grouped[b, j0] = ring.tile([P, PACK * (j1 - j0)], BF16, name="z_grouped", bufs=3, align_bytes=64)
            nc.scalar.copy(
                out=z_grouped[b, j0][:].rearrange("p (c i t) -> p c t i", i=4, t=PACK),
                in_=pages[:, PACK * b * S : PACK * (b + 1) * S]
                .rearrange("p (t m) -> p t m", t=PACK)[:, :, j0:j1]
                .rearrange("p t (c i) -> p c t i", i=4),
            )

        def quantize_z(b, j0, j1):
            z_codes[b, j0] = ring.tile([P, j1 - j0], U32, name="z_codes", bufs=4, align_bytes=64)
            z_scales[b, j0] = ring.tile([P, j1 - j0], U8, name="z_scales", bufs=4, align_bytes=64)
            nc.vector.quantize_mx(
                out=z_codes[b, j0][:].bitcast(FP8X4), scales=z_scales[b, j0][:], in_=z_grouped[b, j0][:]
            )

        def second_product(b, j0, j1, w4_word_sb, w4_scale_sb):
            for c in range(j0 // QUARTER, j1 // QUARTER):
                cols = slice(c * QUARTER - j0, (c + 1) * QUARTER - j0)
                for u in range(N_TILES):
                    nc.tensor.matmul_mx(
                        out=y_banks[c][:, u, :],
                        lhsT=w4_word_sb[:, b, 2 * u * P : 2 * (u + 1) * P].bitcast(FP4X4),
                        lhsT_scale=w4_scale_sb[:, b, u * P : (u + 1) * P],
                        rhs=z_codes[b, j0][:, cols].bitcast(FP8X4),
                        rhs_scale=z_scales[b, j0][:, cols],
                        start=(b == 0 and u == 0),
                        stop=(b == R_PASSES - 1 and u == N_TILES - 1),
                    )

        def finish(c, floors_sb):
            cols = slice(c * QUARTER, (c + 1) * QUARTER)
            held = keep.tile([P, N_TILES, QUARTER], F32, name="held%d" % c)
            nc.vector.tensor_tensor(held[:], y_banks[c][:], floors_sb[:, :, cols], MAX)
            nc.sync.dma_start(out=out.rearrange("(u p) j -> p u j", p=P)[:, :, cols], in_=held[:])

        load_cal(0, keep.tile([P, S], F32, name="cal_first", tag="first", align_bytes=64)[:])
        pages = keep.tile([P, SLICES * S], F32, name="pages", tag="words0", align_bytes=64)
        w1_rest = keep.tile(
            [P, (R_PASSES - 1) * K_PASSES * PACK * PASS + N_TILES * PAIRS], F32, name="w1_rest", tag="words1", align_bytes=64
        )
        for i in range(1, SLICES):
            b, t = divmod(i, PACK)
            if b + 1 < R_PASSES and t == PACK - 1:
                for a in range(K_PASSES):
                    n = b * K_PASSES + a
                    load_w1(b + 1, a, w1_rest[:, n * PACK * PASS : (n + 1) * PACK * PASS])
            load_cal(i, pages[:, LEAD + (i - 1) * S : LEAD + i * S])
        floors_sb = w1_rest[:, (R_PASSES - 1) * K_PASSES * PACK * PASS :].rearrange("p (u j) -> p u j", u=N_TILES)
        nc.sync.dma_start(out=floors_sb, in_=floors.rearrange("(u p) j -> p u j", p=P))
        round_w1(nc.scalar.copy, 0, 0, 0, 1)
        round_w1(nc.scalar.copy, 0, 0, 1, PACK)
        quantize_w1(0, 0, 0, 1)
        round_w1(nc.vector.tensor_copy, 0, 1, 0, 1)
        quantize_w1(0, 1, 0, 1)
        round_w1(nc.vector.tensor_copy, 0, 1, 1, 2)
        round_w1(nc.scalar.copy, 0, 1, 2, PACK)
        quantize_w1(0, 0, 1, PACK)
        quantize_w1(0, 1, 1, 2)
        first_product(0)
        pick_right(0, 0, PAIRS)
        quantize_w1(0, 1, 2, PACK)

        last = SLICES - 1
        for i in range(last):
            b, t = divmod(i, PACK)
            if b + 1 < R_PASSES and t == 0:
                round_w1(nc.scalar.copy, b + 1, 0, 0, PACK)
            if b + 1 < R_PASSES and t == 1:
                quantize_w1(b + 1, 0, 0, PACK)
                round_w1(nc.scalar.copy, b + 1, 1, 0, 1)
                round_w1(nc.scalar.copy, b + 1, 1, 1, PACK)
            if b + 1 < R_PASSES and t == 2:
                quantize_w1(b + 1, 1, 0, 1)
            if b + 1 < R_PASSES and t == 3:
                quantize_w1(b + 1, 1, 1, PACK)
            if b > 0 and t == 1:
                quantize_z(b - 1, 0, PAIRS)
                second_product(b - 1, 0, PAIRS, w4_word_sb, w4_scale_sb)
            first_product(i + 1)
            pick_left(i, 0, PAIRS)
            pick_right(i + 1, 0, PAIRS if i + 1 < last else QUARTER)
            if t == PACK - 1:
                round_z(b, 0, PAIRS)
            if i == PACK - 1:
                w4_word_sb = keep.tile([P, R_PASSES, 2 * N], U8, name="w4_word_sb", tag="mid0", align_bytes=64)
                nc.sync.dma_start(
                    out=w4_word_sb[:].bitcast(I32), in_=w4_words.rearrange("a p n -> p a n").bitcast(I32)
                )
                w4_scale_sb = keep.tile([P, R_PASSES, N], U8, name="w4_scale_sb", tag="mid1", align_bytes=64)
                nc.gpsimd.memset(w4_scale_sb[:].rearrange("p a n -> p (a n)").bitcast(I32), 0)
                for q in range(QUADS):
                    nc.sync.dma_start(
                        out=w4_scale_sb[32 * q : 32 * q + 4, :, :].bitcast(I32),
                        in_=w4_scales[:, 4 * q : 4 * q + 4, :].rearrange("a r n -> r a n").bitcast(I32),
                    )
        b = R_PASSES - 1
        quarters = PAIRS // QUARTER
        for step in range(quarters + 2):
            if step + 1 < quarters:
                pick_right(last, (step + 1) * QUARTER, (step + 2) * QUARTER)
            if step < quarters:
                pick_left(last, step * QUARTER, (step + 1) * QUARTER)
                round_z(b, step * QUARTER, (step + 1) * QUARTER)
            if 1 <= step <= quarters:
                quantize_z(b, (step - 1) * QUARTER, step * QUARTER)
                second_product(b, (step - 1) * QUARTER, step * QUARTER, w4_word_sb, w4_scale_sb)
            if step >= 2:
                finish(step - 2, floors_sb)
